import numpy as np, ml_dtypes
CORES = [16,18,20,22]
N = 4
BF = ml_dtypes.bfloat16
W, A, L, S, Q, C = 4096, 4, 3, 6, 80, 48
def place(x, wv, kv):
    u = np.sum(wv * x, axis=2) & (W - 1)
    return (((u * u) >> 5)[..., None] + kv[:, :, None, :] * u[..., None]) & (W - 1)
def search(X, q, wv, kv):
    n, m = q.shape[0], q.shape[3]
    pl = place(q, wv, kv); ok = np.ones(pl.shape, bool); line = [pl]; levels, dist = [], []
    for l in range(L):
        k = A ** (l + 1)
        occ = np.take_along_axis(X, pl.reshape(n, 8, 1, m * k), 3)
        d = np.sum(np.abs(occ.reshape(n, 8, 16, m, k) - q[..., None]), axis=2)
        if l == 0: hit = np.any(d == 0, axis=3)
        levels.append(pl); dist.append(np.where(ok, d, -1))
        if l < L - 1:
            good = ok & (occ[:, :, 0].reshape(n, 8, m, k) != 512)
            pl = place(occ, wv, kv).reshape(n, 8, m, k * A)
            line = [np.repeat(a, A, axis=3) for a in line]
            ok = np.repeat(good, A, axis=3)
            for a in line: ok = ok & (pl != a)
            line.append(pl)
    D = np.concatenate(dist, axis=3); v = D.shape[3] - 1 - np.argmax(D[..., ::-1], axis=3)
    path = np.full((n, 8, m, L), -1, np.int64); depth = np.zeros((n, 8, m), np.int64); base = 0
    for l in range(L):
        k = A ** (l + 1); here = (v >= base) & (v < base + k); j = np.clip(v - base, 0, k - 1)
        for h in range(l + 1):
            t = np.take_along_axis(levels[h], (j // A ** (l - h))[..., None], 3)[..., 0]
            path[..., h] = np.where(here, t, path[..., h])
        depth = np.where(here, l, depth); base += k
    return (q[:, :, 0] != 512) & ~hit, depth, path
def step(X, q, wv, kv):
    n, m = q.shape[0], q.shape[3]
    live, depth, path = search(X, q, wv, kv)
    meet = np.zeros((n, 8, m, m), bool)
    for a in range(L):
        for b in range(L):
            meet |= (path[..., a][..., :, None] == path[..., b][..., None, :]) & (path[..., a] >= 0)[..., None]
    go = live & ~np.any(meet & live[:, :, None, :] & np.tri(m, m, -1, dtype=bool), axis=3)
    old = [np.take_along_axis(X, np.maximum(path[..., l], 0)[:, :, None, :], 3) for l in range(L)]
    Y = X.copy(); val = q; vic = old[0]
    for l in range(L):
        r, g, i = np.nonzero(go & (depth >= l))
        Y[r, g, :, path[r, g, i, l]] = val[r, g, :, i]; val = old[l]
        vic = np.where((depth >= l)[:, :, None, :], old[l], vic)
    gone = go & (vic[:, :, 0] != 512); slot = np.add.accumulate(gone.astype(np.int64), axis=2) - 1
    out = np.full((n, 8, 16, C), 512, np.int32); r, g, i = np.nonzero(gone & (slot < C))
    out[r, g, :, slot[r, g, i]] = vic[r, g, :, i]
    return Y, out
def records(rng, k): return rng.integers(0, 256, (N, 8, 16, k)).astype(np.int32)
def hashes(rng): return rng.integers(1, 256, (N, 8, 16, 1)).astype(np.int32), 2 * rng.integers(0, 1024, (N, 8, A)) + 1
def fill(rng, rec, wv, kv, full, bare):
    pl = place(rec, wv, kv); k = rec.shape[3]; X = np.full((N, 8, 16, W), 512, np.int32)
    for r in range(N):
        for g in range(8):
            own = np.full(W, -1); free = np.arange(k)
            for a in range(A):
                p = pl[r, g, free, a]; e = own[p] < 0; own[p[e]] = free[e]; free = free[own[p] != free]
            if full[r, g]: own = np.where(own < 0, rng.integers(0, k, W), own)
            own = np.where(rng.random(W) < bare[r, g], -1, own)
            X[r, g] = np.where(own >= 0, rec[r, g][:, own], 512)
    return X
def ask(rng, X, fresh):
    c = rng.integers(0, W, (N, 8, 1, S * Q)); v = np.take_along_axis(X, c, 3).reshape(N, 8, 16, S, Q)
    q = np.where((rng.random((N, 8, 1, S, Q)) < 0.2) & (v[:, :, :1] != 512), v, fresh.reshape(N, 8, 16, S, Q))
    j = np.where(rng.random((N, 8, 1, S, Q)) < 0.06, rng.integers(0, Q, (N, 8, 1, S, Q)), np.arange(Q))
    return np.take_along_axis(q, j, 4)
def pack(X, q, wv, kv):
    return {"x0": X.reshape(N, 128, W).astype(np.float32).astype(BF), "qs": np.ascontiguousarray(q).reshape(N, 128, S * Q).astype(np.float32).astype(BF),
            "wt": wv.reshape(N, 128, 1).astype(np.float32).astype(BF), "kk": np.repeat(kv, 16, axis=1).astype(np.int32)}
def setup_inputs(rng):
    wv, kv = hashes(rng); full = rng.random((N, 8)) < 0.5; bare = rng.choice(np.array([0.0, 0.002, 0.005, 0.02, 0.1]), (N, 8))
    full[:, 0] = True; bare[:, 0] = 0.0; bare[:, 1] = 0.005; bare[:, 2] = 0.02
    X = fill(rng, records(rng, 2 * W), wv, kv, full, bare)
    return pack(X, ask(rng, X, records(rng, S * Q)), wv, kv)
def setup_inputs_room(rng):
    wv, kv = hashes(rng); X = fill(rng, records(rng, 2 * W), wv, kv, np.ones((N, 8), bool), np.zeros((N, 8)))
    q = ask(rng, X, records(rng, S * Q)); pool = records(rng, 2 * Q); live, depth, path = search(X, pool, wv, kv)
    home = np.any(place(X, wv, kv) == np.arange(W)[:, None], axis=3)
    for r in range(N):
        for g in range(8):
            n = int(rng.choice(np.array([0, 1, C - 1, C, C + 1, Q])))
            if r == 0: n = (C, C + 1, Q, C - 1, 1, 0, C, Q)[g]
            used, take = set(), []
            for i in rng.permutation(2 * Q):
                p = set(path[r, g, i].tolist()) - {-1}
                if len(take) < n and live[r, g, i] and not (p & used):
                    take.append(int(i)); used |= p
            stay = rng.choice(np.nonzero(home[r, g])[0], Q - len(take))
            q[r, g, :, 0] = np.concatenate([pool[r, g][:, np.array(take, np.int64)], X[r, g][:, stay]], axis=1)[:, rng.permutation(Q)]
    return pack(X, q, wv, kv)
def setup_inputs_alike(rng):
    wv, kv = hashes(rng); wv[:] = wv[:1].copy(); kv[:, 2] = kv[:, 2, :1]; kv[:, 3, 1:] = kv[:, 3, 1:2]; kv[:] = kv[:1].copy()
    rec = (255 * rng.integers(0, 2, (N, 8, 16, 2 * W))).astype(np.int32); fresh = (255 * rng.integers(0, 2, (N, 8, 16, S * Q))).astype(np.int32)
    few = rng.integers(0, 256, (16, 24)).astype(np.int32)
    for g in (1, 5):
        for r in range(N):
            rec[r, g] = few[:, rng.integers(0, 24, 2 * W)]
            fresh[r, g] = np.where(rng.random(S * Q) < 0.5, few[:, rng.integers(0, 24, S * Q)], rng.integers(0, 256, (16, S * Q)))
    rec[:, 6, :, ::4] = 0
    rec[:, 7] = rng.integers(0, 3, (N, 16, 2 * W))
    full = rng.random((N, 8)) < 0.7; full[:, 1] = True; bare = rng.choice(np.array([0.0, 0.005, 0.02]), (N, 8))
    X = fill(rng, rec, wv, kv, full, bare); q = ask(rng, X, fresh)
    q[:, 4, :, 1] = q[:, 4, :, 1, :1]; q[:, 6, :, 2, ::5] = 0; q[:, 6, :, 0, Q - 1] = 255
    return pack(X, q, wv, kv)
def setup_inputs_hollow(rng):
    wv, kv = hashes(rng); bare = rng.choice(np.array([0.3, 0.6, 0.9, 0.97, 1.0]), (N, 8)); bare[0, 0] = 1.0; bare[1, 1] = 0.6
    full = rng.random((N, 8)) < 0.5; bare[:, 6:] = 0.0; full[:, 7] = True
    X = fill(rng, records(rng, 2 * W), wv, kv, full, bare); q = ask(rng, X, records(rng, S * Q))
    q[:, :, :, 2] = q[:, :, :, 1][..., rng.permutation(Q)]
    return pack(X, q, wv, kv)
def setup_inputs_edges(rng):
    wv, kv = hashes(rng); wv[:, 0] = 255; kv[:, :2] = rng.choice(np.array([1, 2046, 2047]), (N, 2, A)); kv[:, :2, 0] = 2047
    wv[:, 6, 0] |= 1; kv[:, 6] = kv[:, 6, :1].copy()
    full = rng.random((N, 8)) < 0.5; full[:, 0] = True; full[:, 4] = False; full[::2, 5] = True; full[1::2, 5] = False; full[:, 6] = False
    bare = np.zeros((N, 8)); bare[:, 3] = 0.3; bare[:, 7] = 0.1
    rec, fresh = records(rng, 2 * W), records(rng, S * Q)
    for v in (rec, fresh):
        k = v.shape[3]; v[:, 0] = np.where(rng.random((N, 1, k)) < 0.5, rng.integers(200, 256, (N, 16, k)), v[:, 0])
        v[::2, 5] = v[::2, 5] >> 2
    X = fill(rng, rec, wv, kv, full, bare); q = ask(rng, X, fresh)
    q[:, 0, :, 0, 0] = 255
    q[:, 1:3, :, 0, :8] = records(rng, 8)[:, 1:3]
    t = q[:, :, :, 0, :8].copy(); pl = place(t, wv, kv)[..., 0]; i = rng.integers(0, 16, (N, 8, 1, 8))
    near = np.where(np.arange(16)[:, None] == i, t + np.where(t < 255, 1, -1), t)
    for r in range(N):
        for g in (1, 2):
            for j in range(7, -1, -1): X[r, g, :, pl[r, g, j]] = near[r, g, :, j]
    X[:, 3] = np.where(rng.random((N, 1, W)) < 0.02, 0, X[:, 3]); X[:, 3, :, 0] = 512
    q[:, 3, :, 0, 0] = 0; q[:, 3, :, 1, 0] = 255
    X[:, 7, :, 0] = records(rng, 1)[:, 7, :, 0]; q[:, 7, :, 0, 0] = 0; pe = place(X[..., :1], wv, kv)[:, 7, 0]
    for r in range(N): X[r, 7, :, pe[r]] = 512
    for r in range(N):
        g = 4 + r % 2; c = rng.choice(np.nonzero(X[r, g, 0] != 512)[0], Q); q[r, g, :, 0] = X[r, g][:, c]
    q[1::2, 4, :, 0, 0] = records(rng, 1)[1::2, 4, :, 0]; q[1::2, 4, :, 1] = q[1::2, 4, :, 0, :1]
    rr = np.arange(8) % N; m = 256; pool = rng.integers(128, 256, (1, 8, 16, m)).astype(np.int32)
    live, depth, path = search(X[rr, 5][None], pool, wv[rr, 5][None], kv[rr, 5][None])
    for r in range(1, N, 2):
        p = path[0, r]; same = np.sum((p[:, None, :, None] == p[None, :, None, :]) & (p >= 0)[:, None, :, None], axis=(2, 3))
        fit = (same == 1) & live[0, r][:, None] & (live[0, r] & (depth[0, r] == L - 1))[None, :]
        a, b = divmod(int(np.argmax(fit)), m); z = pool[0, r][:, b:b + 1]
        q[r, 5, :, 1] = z; q[r, 5, :, 1, 0] = pool[0, r, :, a]
        X[r - 1, 5] = np.where(rng.random(W) < 0.125, z, X[r - 1, 5])
    mine = place(rec, wv, kv)[:, 6, :, 0]
    for r in range(1, N, 2):
        e = r - 1; p = mine[e]; i = np.nonzero(np.any(X[e, 6][:, p] != rec[e, 6], axis=0))[0]
        i = i[np.unique(p[i], return_index=True)[1]]
        t = place(X[e, 6][:, p[i]][None, None], wv[r:r + 1, 6:7], kv[r:r + 1, 6:7])[0, 0, :, 0]
        j = rng.permutation(np.unique(t, return_index=True)[1]); last = j[X[r, 6, 0, t[j]] != 512][:1]
        j = j[j != last[0]][:Q - 1]; j = np.concatenate([j[:C - 1], last, j[C - 1:]])
        q[e, 6] = rec[e, 6][:, i[j]][:, None, :]
        z = X[r, 6, :, int(t[last[0]])].copy()
        X[r, 6, :, t[j[:C]]] = 512
        c = rng.choice(np.nonzero(X[r, 6, 0] != 512)[0], S * Q); q[r, 6] = X[r, 6][:, c].reshape(16, S, Q); q[r, 6, :, 1, 0] = z
    return pack(X, q, wv, kv)
def setup_inputs_spread(rng):
    def uneven(k):
        v = np.minimum((np.exp2(2 + 6 * rng.random((N, 8, 1, k))) * rng.random((N, 8, 16, k))).astype(np.int32), 255)
        return np.where(rng.random((N, 8, 16, k)) < 0.02, 255, v).astype(np.int32)
    wv = np.minimum(np.exp2(8 * rng.random((N, 8, 16, 1))).astype(np.int32), 255); kv = np.minimum(np.exp2(11 * rng.random((N, 8, A))).astype(np.int64), 2047)
    X = fill(rng, uneven(2 * W), wv, kv, rng.random((N, 8)) < 0.6, rng.choice(np.array([0.0, 0.003, 0.01]), (N, 8)))
    return pack(X, ask(rng, X, uneven(S * Q)), wv, kv)
def check_inputs(d):
    bad = []
    v = np.asarray(d["x0"]).astype(np.float32); e = v == 512
    if not np.all(e | ((v >= 0) & (v <= 255) & (np.floor(v) == v))): bad.append("range of x0")
    e = e.reshape(N, 8, 16, W)
    if np.any(np.any(e, axis=2) != np.all(e, axis=2)): bad.append("empty records of x0")
    for k, lo in (("qs", 0), ("wt", 1)):
        v = np.asarray(d[k]).astype(np.float32)
        if not np.all((v >= lo) & (v <= 255) & (np.floor(v) == v)): bad.append("range of " + k)
    k = np.asarray(d["kk"])
    if np.min(k) < 1 or np.max(k) > 2047: bad.append("range of kk")
    k = k.reshape(N, 8, 16, A)
    if np.any(k != k[:, :, :1]): bad.append("rows of kk")
    return bad
def reference(x0, qs, wt, kk):
    X = x0.astype(np.float32).astype(np.int32).reshape(N, 8, 16, W); q = qs.astype(np.float32).astype(np.int32).reshape(N, 8, 16, S, Q)
    wv = wt.astype(np.float32).astype(np.int32).reshape(N, 8, 16, 1); kv = kk.reshape(N, 8, 16, A)[:, :, 0].astype(np.int64)
    come = np.full((N, 8, 16, C), 512, np.int32)
    for s in range(S):
        X, out = step(X, np.concatenate([q[:, :, :, s], come], axis=3), wv, kv)
        come = np.roll(out, 1, axis=0)
    return {"y": X.reshape(N, 128, W).astype(np.float32).astype(BF)}

from concourse.mybir import AluOpType as A, AxisListType, ActivationFunctionType as F

S, C = 6, 48
NH = {"D": 5, "A": 3}
OFF = {"D": 0, "A": 5}
QC = {"D": 4096, "A": 4256}
DUMPX, XW = 4352, 4736
BIG = 1 << 21
THR = 4090.0 * 128
CM = 12582912.0
ZETA = {"D": (1, 3), "A": (1,)}
LBA = {"D": (1, 3, 5, 7), "A": (1, 3)}
DVC = {"D": (), "A": (1, 2)}
SB, PS = "sbuf", "psum"
CB = ("ID", "NID", "NEG", "BN", "BLK", "TRS", "TRL")
CF = ("PERM", "SCL", "NIF")


def _scratch():
    b, f, i4, u2 = "bfloat16", "float32", "int32", "uint16"
    d = {"X": ([XW], b), "QS": ([480], b), "QXD": ([6 * 1280], b), "QXA": ([768], b), "WT": ([1], b), "KI": ([4], i4), "KF": ([4], f),
         "WL": ([2048], b), "OL": ([2048], b), "CB": ([7 * 128], b), "CF": ([3 * 128], f), "TRR": ([48], b), "HALF": ([240], f),
         "MASK": ([240], f), "RST": ([240], f), "CR": ([240], f), "CG": ([128], f), "CP": ([128], f), "PI": ([4], i4), "PF": ([4], f),
         "GM": ([8], f), "DUMP": ([24], f), "RT": ([8], f), "SD": ([16], f), "GP": ([16], b), "FE": ([384], b), "LB": ([3072], b),
         "SND": ([256], b), "JK": ([2048], b), "RM": ([12], f), "ARR": ([5 * C], b), "r1D": ([24, 20], i4), "r1A": ([4, 12], i4),
         "RG": ([512], b), "s16": ([8], u2)}
    for h in "DA":
        n = NH[h]
        for l, m in ((1, 6 if h == "D" else 1), (2, 4), (3, 16)):
            d["u%s%d" % (h, l)] = ([m, n], i4)
            d["q%s%d" % (h, l)] = ([m, n], i4)
            d["p%s%d" % (h, l)] = ([m, 4 * n], i4)
            d["l%s%d" % (h, l)] = ([m * 4 * n], u2)
        for nm, sh, ty in (("PL", [128 * n], i4), ("e21", [4, 4 * n], b), ("v1r", [4, 4 * n], b), ("v1", [4 * n], b), ("v2", [16 * n], b),
                           ("v2r", [16, 4 * n], b), ("e32", [16, 4 * n], b), ("e31", [16, 4 * n], b), ("d1", [64 * n], b), ("b1", [64 * n], b),
                           ("d2", [256 * n], b), ("b2", [256 * n], b), ("d3", [3 * 256 * n], b), ("cd", [84 * n], b), ("lv", [8 * n], f),
                           ("MI", [n], i4), ("cc", [3 * n], i4), ("co", [3 * n], i4), ("hi", [3 * n], i4), ("o16", [3 * n], u2),
                           ("gm", [48 * n], f), ("sc", [48 * n], f), ("yt", [48 * n], f), ("rl", [4 * n], u2), ("dp", [3 * n], f),
                           ("nc", [3 * n], f), ("wm", [3 * n], f), ("w16", [3 * n], u2), ("res", [3 * n], f)):
            d[nm + h] = (sh, ty)
    o = {k: (SB, [128] + sh, ty) for k, (sh, ty) in d.items()}
    for k in ("UD", "UA", "KD", "KA", "B4", "Z0", "Z1", "Z2"):
        o[k] = (PS, [128, 512], f)
    return o


SCRATCH = _scratch()
BANKS = [k for k in SCRATCH if SCRATCH[k][0] == PS]
SEMAPHORES = ["cV", "cA", "cP", "cG"] + ["m%d" % i for i in range(50)] + ["arr%d" % i for i in range(1, S)] + ["snt%d" % i for i in range(1, S)]
CYC, PCYC, WAKE = 0.00104, 0.0006, 0.1
ORDER = {}


def _dur(q, kind, n):
    if q == "P":
        return n * PCYC
    if kind == "g":
        return 0.06 + 1.5 * n * CYC
    if kind == "s":
        return 0.06 + 3.5 * n * CYC
    return max(64, n) * CYC + (0.06 if q == "A" else 0.0)


def rank_program(g, core, T, topo):
    rank = T.rank_of(core)
    if rank is None:
        return
    v, ac, pe = g.vector, g.scalar, g.tensor
    mc = {nm: T.CB[:, 128 * i:128 * i + 128] for i, nm in enumerate(CB)}
    for i, nm in enumerate(CF):
        mc[nm] = T.CF[:, 128 * i:128 * i + 128]
    ops = []

    def rng(xs):
        return [x if len(x) == 3 else (x[0], 0, 1 << 20) for x in xs]

    def op(q, fn, rd, wr, dur, own=None):
        ops.append((q, fn, rng(rd), rng(wr), dur, own))

    def V(fn, rd, wr, n=64, kind="v"):
        op("V", fn, rd, wr, _dur("V", kind, n))

    def AC(fn, rd, wr, n=64, kind="v"):
        op("A", fn, rd, wr, _dur("A", kind, n))

    def P(fns, rd, wr, n):
        def run():
            i = None
            for f in fns:
                i = f()
            return i
        op("P", run, rd, wr, _dur("P", "p", n))

    nsem = [0]

    def DMA(q, fns, rd, wr, dur):
        name = "m%d" % nsem[0]
        nsem[0] += 1

        def run():
            for f in fns:
                f().then_inc(T.sem[name], 16)
        op(q, run, rd, wr, dur, (name, 16 * len(fns)))

    def mm(out, l, r, a, b):
        return lambda: pe.matmul(out, l, r, a, b)

    def ts(o, i, s1, o1, s2=None, o2=None):
        if o2 is None:
            return lambda: v.tensor_scalar(o, i, s1, None, o1)
        return lambda: v.tensor_scalar(o, i, s1, s2, o1, o2)

    def tt(o, a, b, f):
        return lambda: v.tensor_tensor(out=o, in0=a, in1=b, op=f)

    def cp(o, i):
        return lambda: v.tensor_copy(o, i)

    def ms(o, c):
        return lambda: v.memset(o, c)

    def act(o, i, f, **k):
        return lambda: ac.activation(o, i, f, **k)

    def red(o, i):
        return lambda: v.tensor_reduce(o, i, AxisListType.X, A.max)

    def iota(o, pat, base, wr, n):
        op("G", lambda: g.iota(o, pat, base, 0, allow_small_or_imprecise_dtypes=True), [], [wr], 0.13 + 2 * n * CYC)

    def sd(o, i):
        return lambda: g.sync.dma_start(o, i)

    def W16(t, r):
        return t[:, r * 128:r * 128 + 128]

    DMA("S", [sd(T.QS[:, :], T.qs[:, :]), sd(T.WT[:, :], T.wt[:, :]), sd(T.KI[:, :], T.kk[:, :])], [], [("QS",), ("WT",), ("KI",)], 2.5)
    DMA("AD", [lambda: ac.dma_start(T.X[:, 0:4096], T.x0[:, :])], [], [("X", 0, 4096), ("X0D",)], 6.0)
    op("G", lambda: g.iota(T.PI[:, 0:1], [[0, 1]], 0, 1), [], [("PI", 0, 1)], 0.2)
    iota(T.CG[:, :], [[1, 8], [0, 16]], 0, ("CG",), 128)
    iota(T.CR[:, :], [[0, 15], [1, 16]], 0, ("CR",), 240)
    iota(T.CP[:, :], [[1, 128]], 0, ("CP",), 128)
    V(ts(T.PI[:, 1:2], T.PI[:, 0:1], 4, A.arith_shift_right), [("PI", 0, 1)], [("PI", 1, 2)])
    V(ts(T.PI[:, 2:3], T.PI[:, 0:1], 15, A.bitwise_and), [("PI", 0, 1)], [("PI", 2, 3)])
    V(cp(T.PF[:, 0:3], T.PI[:, 0:3]), [("PI", 0, 3)], [("PF",)])
    pcol, gcol, rcol = T.PF[:, 0:1], T.PF[:, 1:2], T.PF[:, 2:3]
    V(ts(mc["BLK"], T.CG[:, :], gcol, A.is_equal), [("CG",), ("PF",)], [("BLK",)], 128)
    V(ms(T.WL[:, :], 0.0), [], [("WL",)], 1024)
    V(ms(T.OL[:, :], 0.0), [], [("OL",)], 1024)
    for nm, s1, k in (("WL", T.WT[:, 0:1], ("WT",)), ("OL", 128.0, ("BLK",))):
        for r in range(16):
            V(ts(T[nm][:, r * 128 + r:r * 128 + 128:16], T.CB[:, 512:640:16], s1, A.mult), [("BLK",), k] + ([(nm,)] if r == 0 else []), [(nm, r * 128, r * 128 + 128)])
    V(cp(T.KF[:, :], T.KI[:, :]), [("KI",)], [("KF",)])
    V(ts(mc["ID"], T.CP[:, :], pcol, A.is_equal), [("CP",), ("PF",)], [("ID",)], 128)
    for nm, c, n in (("NEG", -float(BIG), 64), ("NID", -1.0, 64), ("BN", float(BIG), 64), ("NIF", -1.0, 128)):
        V(ts(mc[nm], mc["ID"], c, A.mult), [("ID",)], [(nm,)], n)
    V(ts(T.MASK[:, :], T.CR[:, :], rcol, A.is_equal), [("CR",), ("PF",)], [("MASK",)], 240)
    V(ts(T.RST[:, :], T.CR[:, :], 0.0, A.is_gt), [("CR",)], [("RST",)], 240)
    V(ts(mc["TRS"], T.CR[:, 0:128], rcol, A.is_gt), [("CR",), ("PF",)], [("TRS",)], 128)
    V(tt(mc["TRS"], mc["TRS"], mc["BLK"], A.mult), [("TRS",), ("BLK",)], [("TRS",)], 256)
    V(ts(T.TRR[:, :], T.CR[:, 0:48], pcol, A.is_ge, -64.0, A.mult), [("CR",), ("PF",)], [("TRR",)])
    V(ts(T.HALF[:, :], T.CR[:, :], 0.0, A.mult), [("CR",)], [("HALF",)], 240)
    V(ts(T.RM[:, 11:12], rcol, 0.0, A.is_equal, 0.5, A.mult), [("PF",)], [("RM", 11, 12)])
    V(ts(T.HALF[:, :], T.HALF[:, :], T.RM[:, 11:12], A.add), [("HALF",), ("RM", 11, 12)], [("HALF",)], 240)
    for f in range(16):
        V(ms(T.CF[:, 128 + f:256:16], 2.0 ** -(f + 1) if f < 13 else 0.0), [], [("SCL", f, f + 1)])
    V(tt(mc["SCL"], mc["SCL"], mc["BLK"], A.mult), [("SCL",), ("BLK",)], [("SCL",)], 256)
    iota(T.CG[:, :], [[1, 16], [0, 8]], 0, ("CG",), 128)
    iota(T.CP[:, :], [[1, 8], [8, 16]], 0, ("CP",), 128)
    V(ts(mc["TRL"], T.CG[:, :], pcol, A.is_equal), [("CG",), ("PF",)], [("TRL",)], 128)
    V(ts(mc["PERM"], T.CP[:, :], pcol, A.is_equal), [("CP",), ("PF",)], [("PERM",)], 128)
    iota(T.GM[:, :], [[1, 8]], 0, ("GM",), 8)
    V(ts(T.GM[:, :], T.GM[:, :], gcol, A.is_equal), [("GM",), ("PF",)], [("GM",)])
    iota(T.DUMP[:, :], [[16, 24]], DUMPX, ("DUMP",), 24)
    V(ts(T.DUMP[:, :], T.DUMP[:, :], rcol, A.add), [("DUMP",), ("PF",)], [("DUMP",)])
    iota(T.RT[:, :], [[16, 8]], 0, ("RT",), 8)
    V(ts(T.RT[:, :], T.RT[:, :], rcol, A.add), [("RT",), ("PF",)], [("RT",)])
    V(ts(T.SD[:, 0:8], T.RT[:, :], 128.0, A.add), [("RT",)], [("SD", 0, 8)])
    V(ms(T.GP[:, :], 0.0), [], [("GP",)])
    V(ms(T.SND[:, :], 512.0), [], [("SND",)])
    V(ms(T.X[:, 4096:XW], 0.0), [], [("X", 4096, XW)], 320)
    for h in "DA":
        n, o = NH[h], OFF[h]
        for a, b, c in ((0, 4, 4), (4, 20, 16), (20, 84, 64)):
            iota(T["cd" + h][:, a * n:b * n], [[1, b - a], [0, n]], c, ("cd" + h, a * n, b * n), (b - a) * n)
        op("G", (lambda h=h, n=n: g.iota(T["hi" + h][:, :], [[1, n], [0, 3]], 0, 0)), [], [("hi" + h,)], 0.2)
        V(ms(T["PL" + h][:, :], 0), [], [("PL" + h,)], 128 * n)
        for c in range(2):
            V(ts(T["PL" + h][:, c * n:c * n + n], T.RT[:, o:o + n], QC[h] - 16.0 * o + 16 * n * (1 - c), A.add), [("RT",)], [("PL" + h, c * n, c * n + n)])
        k0 = 0 if h == "D" else n
        V(ts(T["rl" + h][:, k0 + 2:k0 + 3 * n:3], T.RT[:, o:o + n], QC[h] - 16.0 * o, A.add), [("RT",)], [("rl" + h, 2, 3)])
        V(ms(T["res" + h][:, :], 0.0), [], [("res" + h,)])

    def chain(h, l, m, c0):
        n, k = NH[h], "%s%d" % (h, l)
        U, u, sq, p = T["U" + h], T["u" + k], T["q" + k], T["p" + k]
        w = m * n
        ru, rq, rp = ("u" + k,), ("q" + k,), ("p" + k,)
        V(cp(u[:, :, :], U[:, c0:c0 + w]), [("U" + h, c0, c0 + w)], [ru], w)
        V(ts(u[:, :, :], u[:, :, :], 4095, A.bitwise_and), [ru], [ru], w)
        V(tt(sq[:, :, :], u[:, :, :], u[:, :, :], A.mult), [ru], [rq], 2 * w)
        for a in range(4):
            V(ts(p[:, :, a * n:a * n + n], u[:, :, :], T.KF[:, a:a + 1], A.mult), [ru, ("KF",)], [("p" + k, a, a + 1)], w)
        V(ts(sq[:, :, :], sq[:, :, :], 5, A.arith_shift_right), [rq], [rq], w)
        for a in range(4):
            pa = p[:, :, a * n:a * n + n]
            V(tt(pa, pa, sq[:, :, :], A.add), [rq, ("p" + k, a, a + 1)], [("p" + k, a, a + 1)], 2 * w)
        V(ts(p[:, :, :], p[:, :, :], 4095, A.bitwise_and), [rp], [rp], 4 * w)
        V(cp(T["l" + k][:, :], p[:, :, :]), [rp], [("l" + k,)], 4 * w)

    def gath(h, l, lc0, oname, o0, QX, qn, q0, w):
        V(tt(T[oname][:, o0:o0 + 16 * w], T.X[:, 0:4096].indirect(T["l%s%d" % (h, l)][:, lc0:lc0 + w]), QX[:, q0:q0 + 16 * w], A.subtract),
          [("X", 0, 4096), ("l%s%d" % (h, l),), (qn, q0, q0 + 16 * w)], [(oname, o0, o0 + 16 * w)], 16 * w, "g")

    def sums(o, L, b, b0, w, a, z):
        return [mm(o, W16(T[L], r), b[:, b0 + r:b0 + 16 * w:16], a and r == 0, z and r == 15) for r in range(16)]

    def keys(h, bname, b0, c0, w, pen, k0=None, code=True, lhs="NEG"):
        k0 = c0 if k0 is None else k0
        o = T["K" + h][:, k0:k0 + w]
        f = sums(o, "OL", T[bname], b0, w, True, False)
        if code:
            f.append(mm(o, mc["ID"], T["cd" + h][:, c0:c0 + w], False, not pen))
        for i, (e, _) in enumerate(pen):
            f.append(mm(o, mc[lhs], e, False, i == len(pen) - 1))
        P(f, [(bname, b0, b0 + 16 * w), ("OL",), ("ID",), (lhs,), ("cd" + h,)] + [x for _, x in pen], [("K" + h, k0, k0 + w)], len(f) * max(64, w))

    zb, jb = [0], [0]

    def bank():
        zb[0] += 1
        return "Z%d" % (zb[0] % 3)

    def search(h, s):
        n = NH[h]
        QX, qn, q0 = (T.QXD, "QXD", s * 1280) if h == "D" else (T.QXA, "QXA", 0)
        U, K, PL, lv = T["U" + h], T["K" + h], T["PL" + h], T["lv" + h]
        un, ln, d3, dn, p2, p3 = "U" + h, "lv" + h, T["d3" + h], "d3" + h, "p%s2" % h, "p%s3" % h
        if h == "A":
            R, rn = T.ARR[:, s * C - C:s * C], "ARR%d" % s
            AC(act(QX[:, 0:48], R, F.Copy), [(rn,)], [(qn, 0, 48)])
            AC(act(QX[:, 48:96], R, F.Copy), [(rn,)], [(qn, 48, 96)])
            w = 96
            while w < 768:
                AC(act(QX[:, w:2 * w], QX[:, 0:w], F.Copy), [(qn, 0, w)], [(qn, w, 2 * w)], w)
                w *= 2
            AC(act(T.X[:, QC[h]:QC[h] + 48], R, F.Copy), [(rn,)], [("X", QC[h], QC[h] + 48)])
            P(sums(U[:, 0:n], "WL", T.ARR, s * C - C, n, True, True) + sums(U[:, n:2 * n], "OL", T.ARR, s * C - C, n, True, True),
              [(rn,), ("WL",), ("OL",)], [(un, 0, 2 * n)], 32 * 64)
            chain("A", 1, 1, 0)
            V(ts(lv[:, 6 * n:7 * n], U[:, n:2 * n], THR, A.is_lt), [(un, n, 2 * n)], [(ln, 6 * n, 7 * n)])
            p1, p1r, l0 = T.pA1[:, 0, :], ("pA1",), 0
        else:
            AC(act(T.X[:, QC[h]:QC[h] + 80], T.QS[:, s * 80:s * 80 + 80], F.Copy), [("QS",)], [("X", QC[h], QC[h] + 80)], 80)
            p1, p1r, l0 = T.pD1[:, s, :], ("pD1",), s * 20
        for l, w, c0, lc in ((1, 4 * n, 32, l0), (2, 16 * n, 64, 0)):
            dd, c1 = "d%d%s" % (l, h), max(64, w) * 16
            P(sums(U[:, c0:c0 + w], "WL", QX, q0, w, True, False), [(qn, q0, q0 + 16 * w), ("WL",)], [(un, c0, c0 + w)], c1)
            gath(h, l, lc, dd, 0, QX, qn, q0, w)
            P(sums(U[:, c0:c0 + w], "WL", T[dd], 0, w, False, True), [(dd,), ("WL",), (un, c0, c0 + w)], [(un, c0, c0 + w)], c1)
            chain(h, l + 1, 4 ** l, c0)
            AC(act(T["b%d%s" % (l, h)][:, :], T[dd][:, :], F.Abs), [(dd,)], [("b%d%s" % (l, h),)], 16 * w)
        keys(h, "b1" + h, 0, 0, 4 * n, [])
        k1 = ("K" + h, 0, 4 * n)
        V(ts(T["v1" + h][:, :], K[:, 0:4 * n], THR, A.is_gt), [k1], [("v1" + h,)])
        V(ts(lv[:, 0:4 * n], K[:, 0:4 * n], 128.0, A.is_ge), [k1], [(ln, 0, 4 * n)])
        V(tt(lv[:, 4 * n:6 * n], lv[:, 0:2 * n], lv[:, 2 * n:4 * n], A.mult), [(ln, 0, 4 * n)], [(ln, 4 * n, 6 * n)])
        V(tt(lv[:, 7 * n:8 * n], lv[:, 4 * n:5 * n], lv[:, 5 * n:6 * n], A.mult), [(ln, 4 * n, 6 * n)], [(ln, 7 * n, 8 * n)])
        if h == "A":
            V(tt(lv[:, 7 * n:8 * n], lv[:, 7 * n:8 * n], lv[:, 6 * n:7 * n], A.mult), [(ln, 6 * n, 8 * n)], [(ln, 7 * n, 8 * n)])
        for a in range(4):
            AC(act(T["v1r" + h][:, :, a * n:a * n + n], T["v1" + h][:, :], F.Copy), [("v1" + h,)], [("v1r" + h, a, a + 1)])
        r1n = "r1A" if h == "A" else "r1D%d" % s
        r1 = T.r1A[:, :, :] if h == "A" else T.r1D[:, 4 * s:4 * s + 4, :]
        if h == "A":
            for a in range(4):
                V(cp(T.r1A[:, :, a * n:a * n + n], p1), [p1r], [("r1A", a, a + 1)])
        up1, up2 = U[:, 288:288 + 16 * n], U[:, 192:192 + 16 * n]
        V(cp(up1, r1), [(r1n,)], [(un, 288, 288 + 16 * n)], 16 * n)
        V(tt(T["e21" + h][:, :, :], T[p2][:, :, :], up1, A.is_equal), [(p2,), (un, 288, 288 + 16 * n)], [("e21" + h,)], 16 * n)
        pen = [(T["e21" + h][:, :, :], ("e21" + h,)), (T["v1r" + h][:, :, :], ("v1r" + h,))]
        keys(h, "b2" + h, 0, 4 * n, 16 * n, pen)
        keys(h, "b2" + h, 0, 4 * n, 16 * n, pen, 84 * n, False, "BN")
        V(ts(T["v2" + h][:, :], K[:, 84 * n:100 * n], THR, A.is_gt), [("K" + h, 84 * n, 100 * n)], [("v2" + h,)], 16 * n)
        for a in range(4):
            AC(act(T["v2r" + h][:, :, a * n:a * n + n], T["v2" + h][:, :], F.Copy), [("v2" + h,)], [("v2r" + h, a, a + 1)], 16 * n)
        V(cp(up2, T[p2][:, :, :]), [(p2,)], [(un, 192, 192 + 16 * n)], 16 * n)
        for a in range(4):
            blk = T[p3][:, :, a * n:a * n + n]
            V(tt(T["e32" + h][:, :, a * n:a * n + n], blk, up2, A.is_equal), [(p3,), (un, 192, 192 + 16 * n)], [("e32" + h, a, a + 1)], 16 * n)
            V(tt(T["e31" + h][:, :, a * n:a * n + n], blk, up1, A.is_equal), [(p3,), (un, 288, 288 + 16 * n)], [("e31" + h, a, a + 1)], 16 * n)
        DMA("S", [sd(PL[:, 4 * n:8 * n], p1), sd(PL[:, 16 * n:32 * n], T[p2][:, :, :]), sd(PL[:, 64 * n:128 * n], T[p3][:, :, :])],
            [p1r, (p2,), (p3,)], [("PL" + h, 4 * n, 8 * n), ("PL" + h, 16 * n, 32 * n), ("PL" + h, 64 * n, 128 * n)], 2.2)
        W, l3 = 256 * n, "l%s3" % h
        for c in range(4):
            b0 = (c % 3) * W
            if c in ZETA[h]:
                AC(act(d3[:, b0:b0 + W], T.X[:, 0:4096].indirect(T[l3][:, c * 16 * n:c * 16 * n + 16 * n]), F.Copy), [("X", 0, 4096), (l3,)], [(dn, b0, b0 + W)], W, "g")
                for a in range(0, W, 512):
                    w = min(512, W - a)
                    Zn = bank()
                    Z, da = T[Zn][:, 0:w], d3[:, b0 + a:b0 + a + w]
                    P([mm(Z, mc["ID"], da, True, False), mm(Z, mc["NID"], QX[:, q0 + a:q0 + a + w], False, True)],
                      [(dn, b0 + a, b0 + a + w), (qn, q0 + a, q0 + a + w), ("ID",), ("NID",)], [(Zn, 0, w)], 2 * w)
                    AC(act(da, Z, F.Abs), [(Zn, 0, w)], [(dn, b0 + a, b0 + a + w)], w)
            else:
                gath(h, 3, c * 16 * n, dn, b0, QX, qn, q0, 16 * n)
                AC(act(d3[:, b0:b0 + W], d3[:, b0:b0 + W], F.Abs), [(dn, b0, b0 + W)], [(dn, b0, b0 + W)], W)
            keys(h, dn, b0, (20 + 16 * c) * n, 16 * n, [(T[e + h][:, 4 * c:4 * c + 4, :], (e + h,)) for e in ("e32", "e31", "v2r")])

    def tail(h, s):
        n, o = NH[h], OFF[h]
        w, f0 = 48 * n, 48 * o
        K, lv, ln, cc, co, gm, sc, yt, rl, dp = [T[x + h] for x in ("K", "lv")] + ["lv" + h] + [T[x + h] for x in ("cc", "co", "gm", "sc", "yt", "rl", "dp")]
        M, rM, live, rlv = lv[:, n:2 * n], (ln, n, 2 * n), lv[:, 7 * n:8 * n], (ln, 7 * n, 8 * n)
        for i in range(n):
            V(red(lv[:, n + i:n + i + 1], K[:, i:84 * n:n]), [("K" + h, 0, 84 * n)], [(ln, n + i, n + i + 1)], 84)
        V(tt(T["MI" + h][:, :], M, live, A.mult), [rM, rlv], [("MI" + h,)])
        for k, (sh, ma) in enumerate(((0, 127), (2, 31), (4, 7))):
            V(ts(cc[:, k:3 * n:3], T["MI" + h][:, :], sh, A.arith_shift_right, ma, A.bitwise_and), [("MI" + h,)], [("cc" + h, k, k + 1)])
        V(ts(co[:, :], cc[:, :], float(n), A.mult), [("cc" + h,)], [("co" + h,)])
        V(tt(co[:, :], co[:, :], T["hi" + h][:, :], A.add), [("co" + h,), ("hi" + h,)], [("co" + h,)])
        V(cp(T["o16" + h][:, :], co[:, :]), [("co" + h,)], [("o16" + h,)])
        V(tt(gm[:, :], T["PL" + h][:, :].indirect(T["o16" + h][:, :]), T.MASK[:, 0:w], A.mult), [("PL" + h,), ("o16" + h,), ("MASK",)], [("gm" + h,)], w, "g")
        P([mm(T.B4[:, 0:w], mc["SCL"], T.HALF[:, 0:w], True, False)], [("SCL",), ("HALF",)], [("B4", 0, w)], 4 * w)
        P([mm(T.B4[:, 0:w], mc["SCL"], gm[:, :], False, True)], [("gm" + h,), ("SCL",), ("B4", 0, w)], [("B4", 0, w)], 4 * w)
        V(lambda: v.tensor_tensor_scan(sc[:, :], T.RST[:, 0:w], gm[:, :], 0.0, A.mult, A.add), [("RST",), ("gm" + h,)], [("sc" + h,)], w)
        k0, v0 = (0, 3 * n) if h == "D" else (n, 0)
        V(cp(rl[:, k0:k0 + 3 * n:3], sc[:, 31:w:48]), [("sc" + h,)], [("rl" + h, 0, 1)])
        V(cp(rl[:, k0 + 1:k0 + 3 * n:3], sc[:, 47:w:48]), [("sc" + h,)], [("rl" + h, 1, 2)])
        V(cp(rl[:, v0:v0 + n], sc[:, 15:w:48]), [("sc" + h,)], [("rl" + h, 3, 4)])
        xw = QC[h] + 32 * n
        AC(act(T.RG[:, 64 * o:64 * o + 64 * n], T.X[:, 0:xw].indirect(rl[:, 0:4 * n]), F.Copy), [("X", 0, xw), ("rl" + h,)], [("RG", 64 * o, 64 * o + 64 * n)], 64 * n, "g")
        ry, fe, rf = ("yt" + h,), T.FE[:, f0:f0 + w], ("FE", f0, f0 + w)
        V(ts(yt[:, :], T.B4[:, 0:w], CM, A.add, CM, A.subtract), [("B4", 0, w)], [ry], w)
        V(tt(yt[:, :], T.B4[:, 0:w], yt[:, :], A.subtract), [("B4", 0, w), ry], [ry], w)
        V(ts(fe, yt[:, :], 0.0, A.is_gt, 0.5, A.subtract), [ry], [rf], w)
        for gg in range(8):
            dst, sg = T.LB[:, f0 * 8 + gg:(f0 + w) * 8:8], T.GM[:, gg:gg + 1]
            if gg in LBA[h]:
                AC(act(dst, fe, F.Copy, scale=sg), [rf, ("GM",)], [("LB" + h, gg, gg + 1)], w)
            else:
                V(ts(dst, fe, sg, A.mult), [rf, ("GM",)], [("LB" + h, gg, gg + 1)], w // 2)
        dmp = T.DUMP[:, 3 * o:3 * o + 3 * n]
        V(tt(dp[:, :], sc[:, 15:w:16], dmp, A.subtract), [("sc" + h,), ("DUMP",)], [("dp" + h,)])
        V(ts(lv[:, 0:n], M, THR, A.is_lt), [rM], [(ln, 0, n)])
        res = T["res" + h]
        for i in range(n):
            gi = o + i
            z = 48 * (gi + 1)
            per = 3 if 3 * z <= 512 else (2 if 2 * z <= 512 else 1)
            for slot, kk in enumerate([list(range(3))[a:a + per] for a in range(0, 3, per)]):
                Zn = bank()
                Z, f, t = T[Zn], [], len(kk) * z
                for j, k in enumerate(kk):
                    L = W16(T.LB, gi * 3 + k)
                    c = j * z
                    if gi:
                        f.append(mm(Z[:, c:c + z - 48], L, T.FE[:, 0:z - 48], True, True))
                    f.append(mm(Z[:, c + z - 48:c + z], L, T.FE[:, z - 48:z], True, False))
                    f.append(mm(Z[:, c + z - 48:c + z], mc["TRL"], T.TRR[:, :], False, True))
                P(f, [("FE", 0, z), ("LB" + h,), ("TRL",), ("TRR",)], [(Zn, 0, t)], len(kk) * (max(64, z - 48) + 128))
                x = slot * n + i
                if slot in DVC[h]:
                    V(red(T.RM[:, x:x + 1], Z[:, 0:t]), [(Zn, 0, t)], [("RM", x, x + 1)], t)
                else:
                    jb[0] = (jb[0] + 512) % 2048
                    j0 = jb[0]
                    AC(act(T.JK[:, j0:j0 + t], Z[:, 0:t], F.Relu, bias=-7.0, scale=2.0, accum_out=res[:, x:x + 1]), [(Zn, 0, t)],
                       [("res" + h, x, x + 1), ("JK", j0, j0 + t)], t)
        if DVC[h]:
            x, y = DVC[h][0] * n, DVC[h][-1] * n + n
            V(ts(res[:, x:y], T.RM[:, x:y], 3.75, A.is_gt), [("RM", x, y)], [("res" + h, x, y)])
        ns = 2 if h == "D" else 3
        c0 = 256 + 16 * (h == "A")
        o4 = T.B4[:, c0:c0 + n]
        P([mm(o4, mc["PERM"], res[:, i * n:i * n + n], i == 0, False) for i in range(ns)] + [mm(o4, mc["NIF"], live, False, True)],
          [("res" + h,), ("PERM",), ("NIF",), rlv], [("B4", c0, c0 + n)], ns * 256 + 256)
        nc, wm = T["nc" + h], T["wm" + h]
        for k in range(3):
            V(ts(nc[:, k:3 * n:3], o4, -1.0, A.is_equal), [("B4", c0, c0 + n)], [("nc" + h, k, k + 1)])
        V(tt(wm[:, :], dp[:, :], nc[:, :], A.mult), [("dp" + h,), ("nc" + h,)], [("wm" + h,)])
        V(tt(wm[:, :], wm[:, :], dmp, A.add), [("wm" + h,), ("DUMP",)], [("wm" + h,)])
        V(cp(T["w16" + h][:, :], wm[:, :]), [("wm" + h,)], [("w16" + h,)])
        if s == S - 1:
            return
        g0 = 8 + o
        V(tt(T.GP[:, g0:g0 + n], nc[:, 0:3 * n:3], lv[:, 0:n], A.mult), [("nc" + h,), (ln, 0, n)], [("GP", g0, g0 + n)])
        if h == "D" and s:
            return
        m = o + n
        gone, rg, ds, p4 = T.GP[:, 8:8 + m], ("GP", 8, 8 + m), T.SD[:, 8:8 + m], T.B4[:, 288:288 + m]
        f = [mm(p4, mc["TRS"], gone, True, False)] + [mm(p4, mc["BLK"], T.GP[:, 8 - x:8 - x + m], False, x == m - 1) for x in range(1, m)]
        P(f, [("GP", 0, 8 + m), ("TRS",), ("BLK",)], [("B4", 288, 288 + m)], 64 * m)
        V(tt(ds, p4, T.SD[:, 0:m], A.subtract), [("B4", 288, 288 + m), ("SD", 0, 8)], [("ds",)])
        V(tt(ds, ds, gone, A.mult), [("ds",), rg], [("ds",)])
        V(tt(ds, ds, T.SD[:, 0:m], A.add), [("ds",), ("SD", 0, 8)], [("ds",)])
        V(cp(T.s16[:, 0:m], ds), [("ds",)], [("s16",)])

    P(sums(T.UD[:, 0:30], "WL", T.QS, 0, 30, True, True), [("QS",), ("WL",)], [("UD", 0, 30)], 1024)
    chain("D", 1, 6, 0)
    for s in range(S):
        b, w = s * 1280, 80
        if s == 0:
            V(cp(T.QXD[:, 0:80], T.QS[:, 0:80]), [("QS",)], [("QXD", 0, 80)])
        else:
            DMA("S", [sd(T.QXD[:, b:b + 80], T.QS[:, s * 80:s * 80 + 80])], [("QS",), ("X0D",)], [("QXD", b, b + 80)], 2.0)
        while w < 1280:
            if s == 0:
                V(cp(T.QXD[:, w:2 * w], T.QXD[:, 0:w]), [("QXD", 0, w)], [("QXD", w, 2 * w)], w // 2)
            else:
                DMA("S", [sd(T.QXD[:, b + w:b + 2 * w], T.QXD[:, b:b + w])], [("QXD", b, b + w)], [("QXD", b + w, b + 2 * w)], 2.0)
            w *= 2
        for a in range(4):
            V(cp(T.r1D[:, 4 * s:4 * s + 4, a * 5:a * 5 + 5], T.pD1[:, s, :]), [("pD1",)], [("r1D%d" % s, a, a + 1)])
    nxt = T.cores[(rank + 1) % len(T.cores)]
    rid, pid = topo.addr(nxt)[:2]
    msk, neng = topo.mask(core, nxt), len(topo.engines(core, nxt))
    for s in range(S):
        halves = "DA" if s else "D"
        if 0 < s < S - 1:
            V(ms(T.SND[:, 0:C], 512.0), [("snt", s, s + 1)], [("SND",)])
        for h in halves:
            search(h, s)
        for h in halves:
            tail(h, s)
        for h in halves:
            n, r0 = NH[h], (0 if h == "D" else 368)
            V((lambda h=h, n=n, r0=r0: v.tensor_copy(T.X[:, :].indirect(T["w16" + h][:, :]), T.RG[:, r0:r0 + 48 * n])),
              [("w16" + h,), ("RG", r0, r0 + 48 * n)], [("X", 0, XW)], 48 * n, "s")
        if s < S - 1:
            n = 8 if s else 5
            V((lambda n=n: v.tensor_copy(T.SND[:, :].indirect(T.s16[:, 0:n]), T.RG[:, 240:240 + 16 * n])), [("s16",), ("RG", 240, 240 + 16 * n)], [("SND",)], 16 * n, "s")
            op("G", (lambda s=s: g.remote_dma(T.ARR[:, s * C:s * C + C], T.SND[:, 0:C], T.sem["arr%d" % (s + 1)], T.sem["snt%d" % (s + 1)], pid, rid, msk)),
               [("SND",)], [], 0.5, ("none", 0))
            op("N", None, [("SND",)], [("ARR%d" % (s + 1),)], 2.5, ("arr%d" % (s + 1), neng))
            op("N", None, [("SND",)], [("snt", s + 1, s + 2)], 2.5, ("snt%d" % (s + 1), neng))
    DMA("S", [sd(T.y[:, 0:2048], T.X[:, 0:2048])], [("X", 0, 2048)], [("y1",)], 4.0)
    DMA("AD", [lambda: ac.dma_start(T.y[:, 2048:4096], T.X[:, 2048:4096])], [("X", 2048, 4096)], [("y2",)], 4.0)

    eng = {"V": v, "A": ac, "P": pe, "G": g, "S": g.sync, "AD": ac}
    phys = {"V": "V", "A": "A", "P": "P", "G": "G", "S": "S", "AD": "A", "N": "N"}
    N = len(ops)
    deps = [dict() for _ in range(N)]
    hist = {}
    for i, (q, fn, rd, wr, du, own) in enumerate(ops):
        for isw, lst in ((0, rd), (1, wr)):
            for nm, lo, hi in lst:
                bank_ = nm in BANKS
                for j, w, a, b in hist.get(nm, ()):
                    over, same = lo < b and a < hi, ops[j][0] == q
                    if j != i and ((over and (isw or w)) or (bank_ and not same)):
                        deps[i][j] = deps[i].get(j, False) or bool(over or not same)
        for isw, lst in ((0, rd), (1, wr)):
            for nm, lo, hi in lst:
                hh = hist.setdefault(nm, [])
                if isw:
                    hh[:] = [x for x in hh if x[0] == i or not (lo <= x[2] and x[3] <= hi)]
                hh.append((i, isw, lo, hi))
    if "o" not in ORDER:
        succ = [[] for _ in range(N)]
        for i in range(N):
            for j in deps[i]:
                succ[j].append(i)
        pri, left, rt, fin = [0.0] * N, [len(d) for d in deps], [0.0] * N, [0.0] * N
        for i in range(N - 1, -1, -1):
            pri[i] = ops[i][4] + max([pri[k] + WAKE for k in succ[i]] + [0.0])
        ready, free, order = {}, {}, []
        for i in range(N):
            if not left[i]:
                ready.setdefault(phys[ops[i][0]], []).append(i)
        while len(order) < N:
            best = None
            for q, lst in ready.items():
                if lst:
                    f = free.get(q, 0.0) if q != "N" else 0.0
                    t0 = min(max(f, rt[i]) for i in lst)
                    c = max((i for i in lst if max(f, rt[i]) <= t0 + 0.03), key=lambda i: (pri[i], -i))
                    t = max(f, rt[c])
                    if best is None or t < best[0]:
                        best = (t, c, q)
            t, c, q = best
            ready[q].remove(c)
            order.append(c)
            free[q] = t + (ops[c][4] if ops[c][0] not in ("S", "AD") else 0.1)
            fin[c] = t + ops[c][4]
            for k in succ[c]:
                left[k] -= 1
                rt[k] = max(rt[k], fin[c] + WAKE * (deps[k][c] is True))
                if not left[k]:
                    ready.setdefault(phys[ops[k][0]], []).append(k)
        ORDER["o"] = order
    cnt = {"V": 0, "A": 0, "P": 0, "G": 0}
    val, snap = [None] * N, [{} for _ in range(N)]
    know = {q: {} for q in "VAPGS"}
    for i in ORDER["o"]:
        q, fn, rd, wr, du, own = ops[i]
        p = phys[q]
        if p == "N":
            val[i] = own
            continue
        kn, want = know[p], {}
        for j, need in deps[i].items():
            if need or p != phys[ops[j][0]]:
                sem, c = val[j]
                if kn.get(sem, 0) < c:
                    want[sem] = max(want.get(sem, (0, 0)), (c, j))
        for sem in sorted(want, key=lambda k: -want[k][1]):
            c, j = want[sem]
            if kn.get(sem, 0) < c:
                eng[q].wait_ge(T.sem[sem], c)
                for k2, c2 in snap[j].items():
                    kn[k2] = max(kn.get(k2, 0), c2)
                kn[sem] = c
        r = fn()
        if own is None:
            cnt[p] += 1
            r.then_inc(T.sem["c" + p], 1)
            val[i] = ("c" + p, cnt[p])
        else:
            val[i] = own
        snap[i] = dict(kn)
    for p in "VAPG":
        g.wait_ge(T.sem["c" + p], cnt[p])
    for i in range(N):
        if ops[i][0] in ("S", "AD"):
            g.wait_ge(T.sem[val[i][0]], val[i][1])
    for s in range(1, S):
        g.wait_ge(T.sem["snt%d" % s], neng)
        g.wait_ge(T.sem["arr%d" % s], neng)
